import numpy as np
import ml_dtypes


def mxq(x, axis, fmt="e4m3"):
    dtype, down = {"e4m3": (ml_dtypes.float8_e4m3fn, 7), "e5m2": (ml_dtypes.float8_e5m2, 14)}[fmt]
    v = np.moveaxis(np.asarray(x, np.float32).astype(ml_dtypes.bfloat16).astype(np.float64), axis, -1)
    blocks = v.reshape(v.shape[:-1] + (-1, 32))
    amax = np.abs(blocks).max(-1, keepdims=True)
    byte = np.maximum(np.where(amax > 0, np.frexp(amax)[1] - 1 + 127, 0) - down, 1)
    scale = np.exp2(byte - 127.0)
    codes = (blocks / scale).astype(np.float32).astype(dtype).astype(np.float64)
    return np.moveaxis((codes * scale).reshape(v.shape), -1, axis)


WIDE = False


def mx_kscale(k):
    if not WIDE:
        return np.ones(k)
    levels = np.array([10, -10, 5, -5, 0])
    if k % 512:
        return np.exp2(np.random.permutation(np.resize(levels, k // 32))).repeat(32)
    a = np.empty((k // 512, 16))
    for p in range(k // 512):
        a[p, :8] = np.random.permutation(np.resize(levels, 8))
        for g in range(8):
            far = levels[np.abs(levels - a[p, g]) >= 10]
            a[p, g + 8] = far[np.random.randint(len(far))]
    return np.exp2(a.ravel()).repeat(32)


def f64(x):
    return np.asarray(x).astype(np.float64)


def striped(idx):
    return np.tile(idx.reshape(-1, 16).T, (8, 1)).astype(np.uint16)


def unstriped(offs):
    return offs[:16].T.reshape(-1).astype(np.int64)


E2M1 = np.array([0.0, 0.5, 1.0, 1.5, 2.0, 3.0, 4.0, 6.0, -0.0, -0.5, -1.0, -1.5, -2.0, -3.0, -4.0, -6.0])


def pack_weight(w, fmt):
    k, n = w.shape
    w = f64(np.asarray(w, np.float32).astype(ml_dtypes.bfloat16)).reshape(k // 32, 32, n)
    amax = np.abs(w).max(1)
    if fmt == "e4m3":
        byte = np.frexp(amax)[1] - 1 + 127 - 7
    else:
        mant, ex = np.frexp(amax / 6.0)
        byte = np.where(mant > 0.5, ex, ex - 1) + 127
    byte = np.clip(np.where(amax > 0, byte, 1), 1, 254)
    scaled = (w * np.exp2(127.0 - byte)[:, None, :]).reshape(k, n).astype(np.float32)
    by_word = np.ascontiguousarray(scaled.reshape(k // 512, 128, 4, n).transpose(0, 1, 3, 2))
    if fmt == "e4m3":
        words = by_word.astype(ml_dtypes.float8_e4m3fn).view(np.uint8)
    else:
        c = by_word.astype(ml_dtypes.float4_e2m1fn).view(np.uint8) & 0xF
        words = (c[..., 0::2] | (c[..., 1::2] << 4)).reshape(k // 512, 128, 2 * n)
    return np.ascontiguousarray(words), np.ascontiguousarray(byte.astype(np.uint8).reshape(k // 512, 16, n))


def unpack_weight(words, scales, fmt):
    g, _, n = scales.shape
    words = np.ascontiguousarray(words).reshape(g, 128, n, -1)
    if fmt == "e4m3":
        vals = words.view(ml_dtypes.float8_e4m3fn).astype(np.float64)
    else:
        nib = np.empty((g, 128, n, 4), np.uint8)
        nib[..., 0::2] = words & 0xF
        nib[..., 1::2] = words >> 4
        vals = E2M1[nib]
    vals = vals * np.repeat(np.exp2(scales.astype(np.float64) - 127.0), 8, axis=1)[..., None]
    return vals.transpose(0, 1, 3, 2).reshape(g * 512, n)


def silu(v):
    return v / (1.0 + np.exp(-np.maximum(v, -700.0)))


K, T, E, C, N = 1536, 512, 12, 128, 256
TOP = 3


def by_expert(wq, xq):
    return np.concatenate([wq[e].T @ xq[:, e * C:(e + 1) * C] for e in range(E)], axis=1)


def setup_inputs():
    n = np.random.standard_normal
    s = mx_kscale(K)[:, None]
    deal = np.repeat(np.arange(E), C).reshape(TOP, T)[:, np.random.permutation(T)]
    deal = np.take_along_axis(deal, np.argsort(np.random.rand(TOP, T), axis=0), axis=0)
    for _ in range(8):
        s_, t_ = np.random.permutation(T).reshape(2, -1); r = np.random.randint(TOP, size=T // 2); x, y = deal[r, s_].copy(), deal[r, t_].copy()
        ok = ~((deal[:, s_] == y).any(0) | (deal[:, t_] == x).any(0)); deal[r[ok], s_[ok]] = y[ok]; deal[r[ok], t_[ok]] = x[ok]
    order = np.lexsort((np.random.rand(TOP * T), deal.reshape(-1)))
    slot_token = order % T; pos = np.empty(TOP * T, np.int64); pos[order] = np.arange(TOP * T); pos = pos.reshape(TOP, T)
    g = np.random.uniform(0.5, 1.5, (TOP, T)); g = g / g.sum(0)
    x = pack_weight(n((K, T)) * s, "e4m3")
    return {
        "x_words": x[0],
        "x_scales": x[1],
        "w": (n((E, K, N)) / np.sqrt(K) / s[None]).astype(np.float32),
        "b": (0.3 * n((N, E))).astype(np.float32),
        "gate": np.stack([np.tile(r, (N, 1)) for r in g]).astype(np.float32),
        "offs": striped(slot_token),
        "pos1": striped(pos[0]),
        "pos2": striped(pos[1]),
        "pos3": striped(pos[2]),
    }


def reference(x_words, x_scales, w, b, gate, offs, pos1, pos2, pos3):
    idx = unstriped(offs)
    xq = unpack_weight(x_words, x_scales, "e4m3")[:, idx]
    y = by_expert(mxq(f64(w), 1, "e4m3"), xq)
    y = silu(y + np.repeat(f64(b), C, axis=1))
    return sum(f64(gate[r]) * y[:, unstriped(p)] for r, p in enumerate((pos1, pos2, pos3)))

@@ -1,0 +1,145 @@
+from contextlib import ExitStack
+
+import concourse.mybir as mybir
+
+K, T, E, C, N = 1536, 512, 12, 128, 256
+TOP = 3
+S = E * C
+P = 128
+PACK = 4
+PASSES = K // (P * PACK)
+BLOCKS = N // P
+GROUP = 3
+FLOPS = 2 * K * N * S
+
+F32 = mybir.dt.float32
+BF16 = mybir.dt.bfloat16
+I32 = mybir.dt.int32
+U32 = mybir.dt.uint32
+U16 = mybir.dt.uint16
+U8 = mybir.dt.uint8
+FP8X4 = mybir.dt.float8_e4m3fn_x4
+SILU = mybir.ActivationFunctionType.Silu
+MULT = mybir.AluOpType.mult
+ADD = mybir.AluOpType.add
+
+
+def tile_moe_pkd_lin_silu_kernel(tc, x_words, x_scales, w, b, gate, offs, pos1, pos2, pos3, out):
+    nc = tc.nc
+    with ExitStack() as ctx:
+        keep = ctx.enter_context(tc.tile_pool(name="keep", bufs=1))
+        raw_pool = ctx.enter_context(tc.tile_pool(name="raw", bufs=E - 1))
+        stage = ctx.enter_context(tc.tile_pool(name="stage", bufs=8))
+        code_pool = ctx.enter_context(tc.tile_pool(name="codes", bufs=9))
+        prod_pool = ctx.enter_context(tc.tile_pool(name="prod", bufs=2))
+        slot_pool = ctx.enter_context(tc.tile_pool(name="slots", bufs=2))
+        psum = ctx.enter_context(tc.psum_pool(name="psum", bufs=6))
+
+        slot_list = keep.tile([P, S // 16], U16, name="slot_list")
+        back_lists = [keep.tile([P, T // 16], U16, name="back_list%d" % r) for r in range(TOP)]
+        token_words = [keep.tile([P, T], I32, name="token_words%d" % o) for o in range(PASSES)]
+        token_scales = keep.tile([P, T], U8, name="token_scales")
+        bias = keep.tile([P, BLOCKS, E], F32, name="bias")
+        results = [keep.tile([P, S], F32, name="results%d" % h) for h in range(BLOCKS)]
+
+        nc.vector.memset(token_scales[:].bitcast(I32), 0)
+        for o in range(PASSES):
+            nc.sync.dma_start(token_words[o][:], x_words[o].rearrange("p t r -> p (t r)").bitcast(I32))
+        nc.sync.dma_start(slot_list[:], offs)
+        for q in range(4):
+            nc.scalar.dma_start(
+                token_scales[32 * q : 32 * q + 4 * PASSES, :].bitcast(I32),
+                x_scales[:, 4 * q : 4 * q + 4, :].bitcast(I32),
+            )
+
+        raw = {}
+        for e in range(E - 1):
+            whole = raw_pool.tile([P, PASSES, PACK, N], F32, name="raw", tag="raw")
+            nc.sync.dma_start(
+                whole[:].rearrange("p o j n -> p o (j n)"),
+                w[e].rearrange("(o p j) n -> p o (j n)", p=P, j=PACK),
+            )
+            for o in range(PASSES):
+                raw[e, o] = whole[:, o]
+            if e == 0:
+                nc.sync.dma_start(bias[:], b.rearrange("(h p) e -> p h e", p=P))
+                for r, pos in enumerate((pos1, pos2, pos3)):
+                    nc.sync.dma_start(back_lists[r][:], pos)
+        for o in range(PASSES):
+            part = keep.tile([P, PACK, N], F32, name="raw_last%d" % o)
+            nc.sync.dma_start(
+                part[:].rearrange("p j n -> p (j n)"),
+                w[E - 1, o * P * PACK : (o + 1) * P * PACK].rearrange("(p j) n -> p (j n)", j=PACK),
+            )
+            raw[E - 1, o] = part[:]
+        gates = raw_pool.tile([P, TOP, T], F32, name="gates", tag="raw")
+        nc.sync.dma_start(gates[:], gate[:, 0:P, :].rearrange("r p t -> p r t"))
+
+        slot_words, slot_scales = {}, {}
+
+        def gather_tokens(g):
+            width = GROUP * C
+            entries = slot_list[:, g * width // 16 : (g + 1) * width // 16]
+            for o in range(PASSES):
+                slot_words[g, o] = slot_pool.tile([P, width], U32, name="slot_words%d" % o, align_bytes=64)
+                nc.vector.tensor_copy(slot_words[g, o][:], token_words[o][:].bitcast(U32).indirect(entries))
+            slot_scales[g] = slot_pool.tile([P, width], U8, name="slot_scales", align_bytes=64)
+            nc.vector.tensor_copy(slot_scales[g][:], token_scales[:].indirect(entries))
+
+        def quantise(rows, on_vector):
+            width = rows.shape[2]
+            grouped = stage.tile([P, width, PACK], BF16, name="grouped", tag="grouped", align_bytes=64)
+            dst = grouped[:].rearrange("p (c i) j -> p c j i", i=4)
+            src = rows.rearrange("p j (c i) -> p c j i", i=4)
+            if on_vector:
+                nc.vector.tensor_copy(dst, src)
+            else:
+                nc.scalar.copy(dst, src)
+            codes = code_pool.tile([P, width], U32, name="codes", tag="codes", align_bytes=64)
+            scales = code_pool.tile([P, width], U8, name="scales", tag="scales", align_bytes=64)
+            nc.vector.quantize_mx(out=codes[:].bitcast(FP8X4), scales=scales[:], in_=grouped[:].rearrange("p n j -> p (n j)"))
+            return codes, scales
+
+        def multiply(e, h, operands):
+            g, c = divmod(e, GROUP)
+            slots = slice(c * C, (c + 1) * C)
+            acc = psum.tile([P, C], F32, name="acc", tag="acc")
+            for o, (codes, scales) in enumerate(operands):
+                nc.tensor.matmul_mx(
+                    out=acc[:],
+                    lhsT=codes.bitcast(FP8X4),
+                    lhsT_scale=scales,
+                    rhs=slot_words[g, o][:, slots].bitcast(FP8X4),
+                    rhs_scale=slot_scales[g][4 * o : P, slots],
+                    start=(o == 0),
+                    stop=(o == PASSES - 1),
+                )
+            nc.scalar.activation(results[h][:, e * C : (e + 1) * C], acc[:], SILU, bias=bias[:, h, e : e + 1])
+
+        for e in range(E):
+            if e % GROUP == 0:
+                gather_tokens(e // GROUP)
+            operands = [[] for h in range(BLOCKS)]
+            for o in range(PASSES):
+                if e == E - 1 and o == PASSES - 1:
+                    for h in range(BLOCKS):
+                        codes, scales = quantise(raw[e, o][:, :, h * P : (h + 1) * P], on_vector=(h == 0))
+                        operands[h].append((codes[:], scales[:]))
+                else:
+                    codes, scales = quantise(raw[e, o], on_vector=(o == PASSES - 1))
+                    for h in range(BLOCKS):
+                        operands[h].append((codes[:, h * P : (h + 1) * P], scales[:, h * P : (h + 1) * P]))
+            for h in range(BLOCKS):
+                multiply(e, h, operands[h])
+
+        for h in range(BLOCKS):
+            terms = []
+            for r in range(TOP):
+                term = prod_pool.tile([P, T], F32, name="term%d" % r)
+                nc.vector.tensor_tensor(term[:], results[h][:].indirect(back_lists[r][:]), gates[:, r, :], MULT)
+                terms.append(term)
+            pair = prod_pool.tile([P, T], F32, name="pair")
+            nc.vector.tensor_tensor(pair[:], terms[0][:], terms[1][:], ADD)
+            total = prod_pool.tile([P, T], F32, name="total")
+            nc.vector.tensor_tensor(total[:], pair[:], terms[2][:], ADD)
+            nc.sync.dma_start(out[h * P : (h + 1) * P, :], total[:])

@@ -1,6 +1,7 @@
 from contextlib import ExitStack
 
 import concourse.mybir as mybir
+from concourse.masks import make_identity
 
 K, T, E, C, N = 1536, 512, 12, 128, 256
 TOP = 3
@@ -9,7 +10,8 @@ P = 128
 PACK = 4
 PASSES = K // (P * PACK)
 BLOCKS = N // P
-GROUP = 3
+AHEAD = 3
+RAW_BYTES = PASSES * PACK * N * 4
 FLOPS = 2 * K * N * S
 
 F32 = mybir.dt.float32
@@ -28,23 +30,24 @@ def tile_moe_pkd_lin_silu_kernel(tc, x_words, x_scales, w, b, gate, offs, pos1, 
     nc = tc.nc
     with ExitStack() as ctx:
         keep = ctx.enter_context(tc.tile_pool(name="keep", bufs=1))
-        raw_pool = ctx.enter_context(tc.tile_pool(name="raw", bufs=E - 1))
-        stage = ctx.enter_context(tc.tile_pool(name="stage", bufs=8))
-        code_pool = ctx.enter_context(tc.tile_pool(name="codes", bufs=9))
-        prod_pool = ctx.enter_context(tc.tile_pool(name="prod", bufs=2))
-        slot_pool = ctx.enter_context(tc.tile_pool(name="slots", bufs=2))
-        psum = ctx.enter_context(tc.psum_pool(name="psum", bufs=6))
+        placed = ctx.enter_context(tc.tile_pool(name="placed", bufs=1))
+        stage = ctx.enter_context(tc.tile_pool(name="stage", bufs=4))
+        code_pool = ctx.enter_context(tc.tile_pool(name="codes", bufs=4))
+        prod_pool = ctx.enter_context(tc.tile_pool(name="prod", bufs=1))
+        psum = ctx.enter_context(tc.psum_pool(name="psum", bufs=8))
 
         slot_list = keep.tile([P, S // 16], U16, name="slot_list")
         back_lists = [keep.tile([P, T // 16], U16, name="back_list%d" % r) for r in range(TOP)]
-        token_words = [keep.tile([P, T], I32, name="token_words%d" % o) for o in range(PASSES)]
+        token_words = keep.tile([P, PASSES, T], I32, name="token_words")
+        identity = keep.tile([P, P], F32, name="identity")
         token_scales = keep.tile([P, T], U8, name="token_scales")
         bias = keep.tile([P, BLOCKS, E], F32, name="bias")
+        gates = keep.tile([P, TOP, T], F32, name="gates")
         results = [keep.tile([P, S], F32, name="results%d" % h) for h in range(BLOCKS)]
 
         nc.vector.memset(token_scales[:].bitcast(I32), 0)
-        for o in range(PASSES):
-            nc.sync.dma_start(token_words[o][:], x_words[o].rearrange("p t r -> p (t r)").bitcast(I32))
+        make_identity(nc, identity[:])
+        nc.sync.dma_start(token_words[:], x_words.rearrange("o p t r -> p o (t r)").bitcast(I32))
         nc.sync.dma_start(slot_list[:], offs)
         for q in range(4):
             nc.scalar.dma_start(
@@ -54,7 +57,7 @@ def tile_moe_pkd_lin_silu_kernel(tc, x_words, x_scales, w, b, gate, offs, pos1, 
 
         raw = {}
         for e in range(E - 1):
-            whole = raw_pool.tile([P, PASSES, PACK, N], F32, name="raw", tag="raw")
+            whole = placed.tile([P, PASSES, PACK, N], F32, name="raw%d" % e, offset=e * RAW_BYTES, align_bytes=64)
             nc.sync.dma_start(
                 whole[:].rearrange("p o j n -> p o (j n)"),
                 w[e].rearrange("(o p j) n -> p o (j n)", p=P, j=PACK),
@@ -63,6 +66,7 @@ def tile_moe_pkd_lin_silu_kernel(tc, x_words, x_scales, w, b, gate, offs, pos1, 
                 raw[e, o] = whole[:, o]
             if e == 0:
                 nc.sync.dma_start(bias[:], b.rearrange("(h p) e -> p h e", p=P))
+            if e == E // 2:
                 for r, pos in enumerate((pos1, pos2, pos3)):
                     nc.sync.dma_start(back_lists[r][:], pos)
         for o in range(PASSES):
@@ -72,74 +76,127 @@ def tile_moe_pkd_lin_silu_kernel(tc, x_words, x_scales, w, b, gate, offs, pos1, 
                 w[E - 1, o * P * PACK : (o + 1) * P * PACK].rearrange("(p j) n -> p (j n)", j=PACK),
             )
             raw[E - 1, o] = part[:]
-        gates = raw_pool.tile([P, TOP, T], F32, name="gates", tag="raw")
         nc.sync.dma_start(gates[:], gate[:, 0:P, :].rearrange("r p t -> p r t"))
 
-        slot_words, slot_scales = {}, {}
+        slot_words, slot_scales, sums = {}, {}, {}
 
-        def gather_tokens(g):
-            width = GROUP * C
-            entries = slot_list[:, g * width // 16 : (g + 1) * width // 16]
+        def slot_tile(e, dtype, index, name):
+            if e < AHEAD:
+                return keep.tile([P, C], dtype, name=name, align_bytes=64)
+            return placed.tile([P, C], dtype, name=name, offset=(e - AHEAD) * RAW_BYTES + index * C * 4, align_bytes=64)
+
+        def gather_tokens(e):
+            entries = slot_list[:, e * C // 16 : (e + 1) * C // 16]
             for o in range(PASSES):
-                slot_words[g, o] = slot_pool.tile([P, width], U32, name="slot_words%d" % o, align_bytes=64)
-                nc.vector.tensor_copy(slot_words[g, o][:], token_words[o][:].bitcast(U32).indirect(entries))
-            slot_scales[g] = slot_pool.tile([P, width], U8, name="slot_scales", align_bytes=64)
-            nc.vector.tensor_copy(slot_scales[g][:], token_scales[:].indirect(entries))
+                slot_words[e, o] = slot_tile(e, U32, o, "slot_words%d_%d" % (e, o))
+                nc.vector.tensor_copy(slot_words[e, o][:], token_words[:, o, :].bitcast(U32).indirect(entries))
+            slot_scales[e] = slot_tile(e, U8, PASSES, "slot_scales%d" % e)
+            nc.vector.tensor_copy(slot_scales[e][:], token_scales[:].indirect(entries))
 
-        def quantise(rows, on_vector):
-            width = rows.shape[2]
-            grouped = stage.tile([P, width, PACK], BF16, name="grouped", tag="grouped", align_bytes=64)
-            dst = grouped[:].rearrange("p (c i) j -> p c j i", i=4)
-            src = rows.rearrange("p j (c i) -> p c j i", i=4)
-            if on_vector:
-                nc.vector.tensor_copy(dst, src)
-            else:
-                nc.scalar.copy(dst, src)
-            codes = code_pool.tile([P, width], U32, name="codes", tag="codes", align_bytes=64)
-            scales = code_pool.tile([P, width], U8, name="scales", tag="scales", align_bytes=64)
-            nc.vector.quantize_mx(out=codes[:].bitcast(FP8X4), scales=scales[:], in_=grouped[:].rearrange("p n j -> p (n j)"))
+        def interleave(copy, grouped, rows):
+            copy(grouped.rearrange("p (c i) j -> p c j i", i=4), rows.rearrange("p j (c i) -> p c j i", i=4))
+
+        def quantise(grouped, tag):
+            width = grouped.shape[1]
+            codes = code_pool.tile([P, width], U32, name="codes", tag="codes" + tag, align_bytes=64)
+            scales = code_pool.tile([P, width], U8, name="scales", tag="scales" + tag, align_bytes=64)
+            nc.vector.quantize_mx(out=codes[:].bitcast(FP8X4), scales=scales[:], in_=grouped.rearrange("p n j -> p (n j)"))
             return codes, scales
 
-        def multiply(e, h, operands):
-            g, c = divmod(e, GROUP)
-            slots = slice(c * C, (c + 1) * C)
-            acc = psum.tile([P, C], F32, name="acc", tag="acc")
-            for o, (codes, scales) in enumerate(operands):
-                nc.tensor.matmul_mx(
-                    out=acc[:],
-                    lhsT=codes.bitcast(FP8X4),
-                    lhsT_scale=scales,
-                    rhs=slot_words[g, o][:, slots].bitcast(FP8X4),
-                    rhs_scale=slot_scales[g][4 * o : P, slots],
-                    start=(o == 0),
-                    stop=(o == PASSES - 1),
-                )
-            nc.scalar.activation(results[h][:, e * C : (e + 1) * C], acc[:], SILU, bias=bias[:, h, e : e + 1])
+        def multiply(e, o, h, quantised, first):
+            codes, scales = quantised
+            if o == 0:
+                sums[e, h] = psum.tile([P, C], F32, name="acc", tag="acc")
+            nc.tensor.matmul_mx(
+                out=sums[e, h][:],
+                lhsT=codes[:, first : first + P].bitcast(FP8X4),
+                lhsT_scale=scales[:, first : first + P],
+                rhs=slot_words[e, o][:].bitcast(FP8X4),
+                rhs_scale=slot_scales[e][4 * o : P, :],
+                start=(o == 0),
+                stop=(o == PASSES - 1),
+            )
 
-        for e in range(E):
-            if e % GROUP == 0:
-                gather_tokens(e // GROUP)
-            operands = [[] for h in range(BLOCKS)]
-            for o in range(PASSES):
-                if e == E - 1 and o == PASSES - 1:
-                    for h in range(BLOCKS):
-                        codes, scales = quantise(raw[e, o][:, :, h * P : (h + 1) * P], on_vector=(h == 0))
-                        operands[h].append((codes[:], scales[:]))
-                else:
-                    codes, scales = quantise(raw[e, o], on_vector=(o == PASSES - 1))
-                    for h in range(BLOCKS):
-                        operands[h].append((codes[:, h * P : (h + 1) * P], scales[:, h * P : (h + 1) * P]))
+        def activate(e, h):
+            nc.scalar.activation(results[h][:, e * C : (e + 1) * C], sums[e, h][:], SILU, bias=bias[:, h, e : e + 1])
+
+        for e in range(AHEAD):
+            gather_tokens(e)
+        def single_tile(width):
+            return stage.tile([P, width, PACK], BF16, name="single", tag="single", align_bytes=64)
+
+        def pair_tile():
+            return stage.tile([P, 2 * N, PACK], BF16, name="pair", tag="pair", align_bytes=64)
+
+        def multiply_blocks(e, o, quantised, first):
             for h in range(BLOCKS):
-                multiply(e, h, operands[h])
+                multiply(e, o, h, quantised, first + h * P)
 
+        last = E - 1
+        pair = pair_tile()
+        for e in range(last):
+            single = single_tile(N)
+            interleave(nc.scalar.copy, pair[:, N:, :], raw[e, 0])
+            interleave(nc.scalar.copy, single[:], raw[e, 1])
+            next_pair = pair_tile()
+            interleave(nc.vector.tensor_copy, next_pair[:, :N, :], raw[e, 2])
+            if e == 0:
+                multiply_blocks(e, 0, quantise(pair[:, N:, :], "single"), 0)
+            else:
+                quantised = quantise(pair[:], "pair")
+                multiply_blocks(e - 1, 2, quantised, 0)
+                multiply_blocks(e, 0, quantised, N)
+                for h in range(BLOCKS):
+                    activate(e - 1, h)
+            multiply_blocks(e, 1, quantise(single[:], "single"), 0)
+            if e + AHEAD < E:
+                gather_tokens(e + AHEAD)
+            pair = next_pair
+        multiply_blocks(last - 1, 2, quantise(pair[:, :N, :], "single"), 0)
         for h in range(BLOCKS):
-            terms = []
-            for r in range(TOP):
-                term = prod_pool.tile([P, T], F32, name="term%d" % r)
-                nc.vector.tensor_tensor(term[:], results[h][:].indirect(back_lists[r][:]), gates[:, r, :], MULT)
-                terms.append(term)
-            pair = prod_pool.tile([P, T], F32, name="pair")
-            nc.vector.tensor_tensor(pair[:], terms[0][:], terms[1][:], ADD)
-            total = prod_pool.tile([P, T], F32, name="total")
-            nc.vector.tensor_tensor(total[:], pair[:], terms[2][:], ADD)
-            nc.sync.dma_start(out[h * P : (h + 1) * P, :], total[:])
+            activate(last - 1, h)
+        for o, copy in enumerate((nc.scalar.copy, nc.vector.tensor_copy)):
+            single = single_tile(N)
+            interleave(copy, single[:], raw[last, o])
+            multiply_blocks(last, o, quantise(single[:], "single"), 0)
+        halves = [single_tile(P) for h in range(BLOCKS)]
+        for h, copy in enumerate((nc.scalar.copy, nc.vector.tensor_copy)):
+            interleave(copy, halves[h][:], raw[last, 2][:, :, h * P : (h + 1) * P])
+        for h in range(BLOCKS):
+            multiply(last, 2, h, quantise(halves[h][:], "single"), 0)
+            activate(last, h)
+
+        def gated(h, r, tokens, name):
+            width = tokens.stop - tokens.start
+            term = prod_pool.tile([P, width], F32, name=name)
+            entries = back_lists[r][:, tokens.start // 16 : tokens.stop // 16]
+            nc.vector.tensor_tensor(term[:], results[h][:].indirect(entries), gates[:, r, tokens], MULT)
+            return term
+
+        turned = [psum.tile([P, P], F32, name="acc", tag="acc") for i in range(T // P)]
+        for r in range(TOP):
+            term = gated(0, r, slice(0, T), "first%d" % r)
+            for i in range(T // P):
+                nc.tensor.matmul(
+                    turned[i][:], term[:, i * P : (i + 1) * P], identity[:],
+                    start=(r == 0), stop=(r == TOP - 1), is_transpose=True,
+                )
+        back = psum.tile([P, T], F32, name="acc", tag="acc")
+        for i in range(T // P):
+            by_token = prod_pool.tile([P, P], F32, name="by_token%d" % i)
+            nc.scalar.copy(by_token[:], turned[i][:])
+            nc.tensor.transpose(back[:, i * P : (i + 1) * P], by_token[:], identity[:])
+        total = prod_pool.tile([P, T], F32, name="total")
+        nc.scalar.copy(total[:], back[:])
+        nc.sync.dma_start(out[0:P, :], total[:])
+
+        left, right = slice(0, T // 2), slice(T // 2, T)
+        terms = [gated(1, r, slice(0, T), "second%d" % r) for r in range(TOP - 1)]
+        third_left = gated(1, TOP - 1, left, "third_left")
+        partial = prod_pool.tile([P, T], F32, name="partial")
+        nc.vector.tensor_tensor(partial[:], terms[0][:], terms[1][:], ADD)
+        third_right = gated(1, TOP - 1, right, "third_right")
+        for name, tokens, third in (("left", left, third_left), ("right", right, third_right)):
+            done = prod_pool.tile([P, T // 2], F32, name=name)
+            nc.vector.tensor_tensor(done[:], partial[:, tokens], third[:], ADD)
+            nc.sync.dma_start(out[P : 2 * P, tokens], done[:])

@@ -10,7 +10,9 @@ P = 128
 PACK = 4
 PASSES = K // (P * PACK)
 BLOCKS = N // P
-AHEAD = 3
+GROUP = 3
+EARLY = 7
+WHOLE = E - 2
 RAW_BYTES = PASSES * PACK * N * 4
 FLOPS = 2 * K * N * S
 
@@ -38,17 +40,18 @@ def tile_moe_pkd_lin_silu_kernel(tc, x_words, x_scales, w, b, gate, offs, pos1, 
 
         slot_list = keep.tile([P, S // 16], U16, name="slot_list")
         back_lists = [keep.tile([P, T // 16], U16, name="back_list%d" % r) for r in range(TOP)]
-        token_words = keep.tile([P, PASSES, T], I32, name="token_words")
+        token_words = [keep.tile([P, T], I32, name="token_words%d" % o) for o in range(PASSES)]
         identity = keep.tile([P, P], F32, name="identity")
         token_scales = keep.tile([P, T], U8, name="token_scales")
         bias = keep.tile([P, BLOCKS, E], F32, name="bias")
-        gates = keep.tile([P, TOP, T], F32, name="gates")
+        gates = [keep.tile([P, T], F32, name="gates%d" % r) for r in range(TOP)]
         results = [keep.tile([P, S], F32, name="results%d" % h) for h in range(BLOCKS)]
 
-        nc.vector.memset(token_scales[:].bitcast(I32), 0)
+        nc.gpsimd.memset(token_scales[:].bitcast(I32), 0)
         make_identity(nc, identity[:])
-        nc.sync.dma_start(token_words[:], x_words.rearrange("o p t r -> p o (t r)").bitcast(I32))
         nc.sync.dma_start(slot_list[:], offs)
+        for o in range(PASSES):
+            nc.sync.dma_start(token_words[o][:], x_words[o].rearrange("p t r -> p (t r)").bitcast(I32))
         for q in range(4):
             nc.scalar.dma_start(
                 token_scales[32 * q : 32 * q + 4 * PASSES, :].bitcast(I32),
@@ -56,7 +59,7 @@ def tile_moe_pkd_lin_silu_kernel(tc, x_words, x_scales, w, b, gate, offs, pos1, 
             )
 
         raw = {}
-        for e in range(E - 1):
+        for e in range(WHOLE):
             whole = placed.tile([P, PASSES, PACK, N], F32, name="raw%d" % e, offset=e * RAW_BYTES, align_bytes=64)
             nc.sync.dma_start(
                 whole[:].rearrange("p o j n -> p o (j n)"),
@@ -69,29 +72,32 @@ def tile_moe_pkd_lin_silu_kernel(tc, x_words, x_scales, w, b, gate, offs, pos1, 
             if e == E // 2:
                 for r, pos in enumerate((pos1, pos2, pos3)):
                     nc.sync.dma_start(back_lists[r][:], pos)
-        for o in range(PASSES):
-            part = keep.tile([P, PACK, N], F32, name="raw_last%d" % o)
-            nc.sync.dma_start(
-                part[:].rearrange("p j n -> p (j n)"),
-                w[E - 1, o * P * PACK : (o + 1) * P * PACK].rearrange("(p j) n -> p (j n)", j=PACK),
-            )
-            raw[E - 1, o] = part[:]
-        nc.sync.dma_start(gates[:], gate[:, 0:P, :].rearrange("r p t -> p r t"))
-
-        slot_words, slot_scales, sums = {}, {}, {}
-
-        def slot_tile(e, dtype, index, name):
-            if e < AHEAD:
-                return keep.tile([P, C], dtype, name=name, align_bytes=64)
-            return placed.tile([P, C], dtype, name=name, offset=(e - AHEAD) * RAW_BYTES + index * C * 4, align_bytes=64)
-
-        def gather_tokens(e):
-            entries = slot_list[:, e * C // 16 : (e + 1) * C // 16]
+        for e in range(WHOLE, E):
             for o in range(PASSES):
-                slot_words[e, o] = slot_tile(e, U32, o, "slot_words%d_%d" % (e, o))
-                nc.vector.tensor_copy(slot_words[e, o][:], token_words[:, o, :].bitcast(U32).indirect(entries))
-            slot_scales[e] = slot_tile(e, U8, PASSES, "slot_scales%d" % e)
-            nc.vector.tensor_copy(slot_scales[e][:], token_scales[:].indirect(entries))
+                part = keep.tile([P, PACK, N], F32, name="raw%d_%d" % (e, o))
+                nc.sync.dma_start(
+                    part[:].rearrange("p j n -> p (j n)"),
+                    w[e, o * P * PACK : (o + 1) * P * PACK].rearrange("(p j) n -> p (j n)", j=PACK),
+                )
+                raw[e, o] = part[:]
+        for r in range(TOP):
+            nc.sync.dma_start(gates[r][:], gate[r, 0:P, :])
+
+        gathered, sums = {}, {}
+        gathers = [(g, part) for g in range(E // GROUP) for part in (0, PASSES, 1, 2)]
+
+        def gather_tokens(index):
+            g, part = gathers[index]
+            width = GROUP * C
+            dtype = U32 if part < PASSES else U8
+            window = token_words[part][:].bitcast(U32) if part < PASSES else token_scales[:]
+            name = "gathered%d" % index
+            if index < EARLY:
+                tile = keep.tile([P, width], dtype, name=name, align_bytes=64)
+            else:
+                tile = placed.tile([P, width], dtype, name=name, offset=(index - EARLY) * RAW_BYTES, align_bytes=64)
+            nc.vector.tensor_copy(tile[:], window.indirect(slot_list[:, g * width // 16 : (g + 1) * width // 16]))
+            gathered[g, part] = tile
 
         def interleave(copy, grouped, rows):
             copy(grouped.rearrange("p (c i) j -> p c j i", i=4), rows.rearrange("p j (c i) -> p c j i", i=4))
@@ -105,14 +111,16 @@ def tile_moe_pkd_lin_silu_kernel(tc, x_words, x_scales, w, b, gate, offs, pos1, 
 
         def multiply(e, o, h, quantised, first):
             codes, scales = quantised
+            g, c = divmod(e, GROUP)
+            slots = slice(c * C, (c + 1) * C)
             if o == 0:
                 sums[e, h] = psum.tile([P, C], F32, name="acc", tag="acc")
             nc.tensor.matmul_mx(
                 out=sums[e, h][:],
                 lhsT=codes[:, first : first + P].bitcast(FP8X4),
                 lhsT_scale=scales[:, first : first + P],
-                rhs=slot_words[e, o][:].bitcast(FP8X4),
-                rhs_scale=slot_scales[e][4 * o : P, :],
+                rhs=gathered[g, o][:, slots].bitcast(FP8X4),
+                rhs_scale=gathered[g, PASSES][4 * o : P, slots],
                 start=(o == 0),
                 stop=(o == PASSES - 1),
             )
@@ -120,8 +128,8 @@ def tile_moe_pkd_lin_silu_kernel(tc, x_words, x_scales, w, b, gate, offs, pos1, 
         def activate(e, h):
             nc.scalar.activation(results[h][:, e * C : (e + 1) * C], sums[e, h][:], SILU, bias=bias[:, h, e : e + 1])
 
-        for e in range(AHEAD):
-            gather_tokens(e)
+        for index in range(EARLY):
+            gather_tokens(index)
         def single_tile(width):
             return stage.tile([P, width, PACK], BF16, name="single", tag="single", align_bytes=64)
 
@@ -134,7 +142,7 @@ def tile_moe_pkd_lin_silu_kernel(tc, x_words, x_scales, w, b, gate, offs, pos1, 
 
         last = E - 1
         pair = pair_tile()
-        for e in range(last):
+        for e in range(WHOLE):
             single = single_tile(N)
             interleave(nc.scalar.copy, pair[:, N:, :], raw[e, 0])
             interleave(nc.scalar.copy, single[:], raw[e, 1])
@@ -149,16 +157,23 @@ def tile_moe_pkd_lin_silu_kernel(tc, x_words, x_scales, w, b, gate, offs, pos1, 
                 for h in range(BLOCKS):
                     activate(e - 1, h)
             multiply_blocks(e, 1, quantise(single[:], "single"), 0)
-            if e + AHEAD < E:
-                gather_tokens(e + AHEAD)
+            if e + EARLY < len(gathers):
+                gather_tokens(e + EARLY)
             pair = next_pair
-        multiply_blocks(last - 1, 2, quantise(pair[:, :N, :], "single"), 0)
+        interleave(nc.vector.tensor_copy, pair[:, N:, :], raw[WHOLE, 0])
+        quantised = quantise(pair[:], "pair")
+        multiply_blocks(WHOLE - 1, 2, quantised, 0)
+        multiply_blocks(WHOLE, 0, quantised, N)
         for h in range(BLOCKS):
-            activate(last - 1, h)
-        for o, copy in enumerate((nc.scalar.copy, nc.vector.tensor_copy)):
+            activate(WHOLE - 1, h)
+        for index in range(WHOLE * PASSES + 1, E * PASSES - 1):
+            e, o = divmod(index, PASSES)
             single = single_tile(N)
-            interleave(copy, single[:], raw[last, o])
-            multiply_blocks(last, o, quantise(single[:], "single"), 0)
+            interleave(nc.scalar.copy if index % 2 else nc.vector.tensor_copy, single[:], raw[e, o])
+            multiply_blocks(e, o, quantise(single[:], "single"), 0)
+            if o == PASSES - 1:
+                for h in range(BLOCKS):
+                    activate(e, h)
         halves = [single_tile(P) for h in range(BLOCKS)]
         for h, copy in enumerate((nc.scalar.copy, nc.vector.tensor_copy)):
             interleave(copy, halves[h][:], raw[last, 2][:, :, h * P : (h + 1) * P])
@@ -170,7 +185,7 @@ def tile_moe_pkd_lin_silu_kernel(tc, x_words, x_scales, w, b, gate, offs, pos1, 
             width = tokens.stop - tokens.start
             term = prod_pool.tile([P, width], F32, name=name)
             entries = back_lists[r][:, tokens.start // 16 : tokens.stop // 16]
-            nc.vector.tensor_tensor(term[:], results[h][:].indirect(entries), gates[:, r, tokens], MULT)
+            nc.vector.tensor_tensor(term[:], results[h][:].indirect(entries), gates[r][:, tokens], MULT)
             return term
 
         turned = [psum.tile([P, P], F32, name="acc", tag="acc") for i in range(T // P)]

from contextlib import ExitStack

import concourse.mybir as mybir
from concourse.masks import make_identity

K, T, E, C, N = 1536, 512, 12, 128, 256
TOP = 3
S = E * C
P = 128
PACK = 4
PASSES = K // (P * PACK)
BLOCKS = N // P
GROUP = 3
EARLY = 7
WHOLE = E - 2
RAW_BYTES = PASSES * PACK * N * 4
FLOPS = 2 * K * N * S

F32 = mybir.dt.float32
BF16 = mybir.dt.bfloat16
I32 = mybir.dt.int32
U32 = mybir.dt.uint32
U16 = mybir.dt.uint16
U8 = mybir.dt.uint8
FP8X4 = mybir.dt.float8_e4m3fn_x4
SILU = mybir.ActivationFunctionType.Silu
MULT = mybir.AluOpType.mult
ADD = mybir.AluOpType.add


def tile_moe_pkd_lin_silu_kernel(tc, x_words, x_scales, w, b, gate, offs, pos1, pos2, pos3, out):
    nc = tc.nc
    with ExitStack() as ctx:
        keep = ctx.enter_context(tc.tile_pool(name="keep", bufs=1))
        placed = ctx.enter_context(tc.tile_pool(name="placed", bufs=1))
        stage = ctx.enter_context(tc.tile_pool(name="stage", bufs=4))
        code_pool = ctx.enter_context(tc.tile_pool(name="codes", bufs=4))
        prod_pool = ctx.enter_context(tc.tile_pool(name="prod", bufs=1))
        psum = ctx.enter_context(tc.psum_pool(name="psum", bufs=8))

        slot_list = keep.tile([P, S // 16], U16, name="slot_list")
        back_lists = [keep.tile([P, T // 16], U16, name="back_list%d" % r) for r in range(TOP)]
        token_words = [keep.tile([P, T], I32, name="token_words%d" % o) for o in range(PASSES)]
        identity = keep.tile([P, P], F32, name="identity")
        token_scales = keep.tile([P, T], U8, name="token_scales")
        bias = keep.tile([P, BLOCKS, E], F32, name="bias")
        gates = [keep.tile([P, T], F32, name="gates%d" % r) for r in range(TOP)]
        results = [keep.tile([P, S], F32, name="results%d" % h) for h in range(BLOCKS)]

        nc.gpsimd.memset(token_scales[:].bitcast(I32), 0)
        make_identity(nc, identity[:])
        nc.sync.dma_start(slot_list[:], offs)
        for o in range(PASSES):
            nc.sync.dma_start(token_words[o][:], x_words[o].rearrange("p t r -> p (t r)").bitcast(I32))
        for q in range(4):
            nc.scalar.dma_start(
                token_scales[32 * q : 32 * q + 4 * PASSES, :].bitcast(I32),
                x_scales[:, 4 * q : 4 * q + 4, :].bitcast(I32),
            )

        raw = {}
        for e in range(WHOLE):
            whole = placed.tile([P, PASSES, PACK, N], F32, name="raw%d" % e, offset=e * RAW_BYTES, align_bytes=64)
            nc.sync.dma_start(
                whole[:].rearrange("p o j n -> p o (j n)"),
                w[e].rearrange("(o p j) n -> p o (j n)", p=P, j=PACK),
            )
            for o in range(PASSES):
                raw[e, o] = whole[:, o]
            if e == 0:
                nc.sync.dma_start(bias[:], b.rearrange("(h p) e -> p h e", p=P))
            if e == E // 2:
                for r, pos in enumerate((pos1, pos2, pos3)):
                    nc.sync.dma_start(back_lists[r][:], pos)
        for e in range(WHOLE, E):
            for o in range(PASSES):
                part = keep.tile([P, PACK, N], F32, name="raw%d_%d" % (e, o))
                nc.sync.dma_start(
                    part[:].rearrange("p j n -> p (j n)"),
                    w[e, o * P * PACK : (o + 1) * P * PACK].rearrange("(p j) n -> p (j n)", j=PACK),
                )
                raw[e, o] = part[:]
        for r in range(TOP):
            nc.sync.dma_start(gates[r][:], gate[r, 0:P, :])

        gathered, sums = {}, {}
        gathers = [(g, part) for g in range(E // GROUP) for part in (0, PASSES, 1, 2)]

        def gather_tokens(index):
            g, part = gathers[index]
            width = GROUP * C
            dtype = U32 if part < PASSES else U8
            window = token_words[part][:].bitcast(U32) if part < PASSES else token_scales[:]
            name = "gathered%d" % index
            if index < EARLY:
                tile = keep.tile([P, width], dtype, name=name, align_bytes=64)
            else:
                tile = placed.tile([P, width], dtype, name=name, offset=(index - EARLY) * RAW_BYTES, align_bytes=64)
            nc.vector.tensor_copy(tile[:], window.indirect(slot_list[:, g * width // 16 : (g + 1) * width // 16]))
            gathered[g, part] = tile

        def interleave(copy, grouped, rows):
            copy(grouped.rearrange("p (c i) j -> p c j i", i=4), rows.rearrange("p j (c i) -> p c j i", i=4))

        def quantise(grouped, tag):
            width = grouped.shape[1]
            codes = code_pool.tile([P, width], U32, name="codes", tag="codes" + tag, align_bytes=64)
            scales = code_pool.tile([P, width], U8, name="scales", tag="scales" + tag, align_bytes=64)
            nc.vector.quantize_mx(out=codes[:].bitcast(FP8X4), scales=scales[:], in_=grouped.rearrange("p n j -> p (n j)"))
            return codes, scales

        def multiply(e, o, h, quantised, first):
            codes, scales = quantised
            g, c = divmod(e, GROUP)
            slots = slice(c * C, (c + 1) * C)
            if o == 0:
                sums[e, h] = psum.tile([P, C], F32, name="acc", tag="acc")
            nc.tensor.matmul_mx(
                out=sums[e, h][:],
                lhsT=codes[:, first : first + P].bitcast(FP8X4),
                lhsT_scale=scales[:, first : first + P],
                rhs=gathered[g, o][:, slots].bitcast(FP8X4),
                rhs_scale=gathered[g, PASSES][4 * o : P, slots],
                start=(o == 0),
                stop=(o == PASSES - 1),
            )

        def activate(e, h):
            nc.scalar.activation(results[h][:, e * C : (e + 1) * C], sums[e, h][:], SILU, bias=bias[:, h, e : e + 1])

        for index in range(EARLY):
            gather_tokens(index)
        def single_tile(width):
            return stage.tile([P, width, PACK], BF16, name="single", tag="single", align_bytes=64)

        def pair_tile():
            return stage.tile([P, 2 * N, PACK], BF16, name="pair", tag="pair", align_bytes=64)

        def multiply_blocks(e, o, quantised, first):
            for h in range(BLOCKS):
                multiply(e, o, h, quantised, first + h * P)

        last = E - 1
        pair = pair_tile()
        for e in range(WHOLE):
            single = single_tile(N)
            interleave(nc.scalar.copy, pair[:, N:, :], raw[e, 0])
            interleave(nc.scalar.copy, single[:], raw[e, 1])
            next_pair = pair_tile()
            interleave(nc.vector.tensor_copy, next_pair[:, :N, :], raw[e, 2])
            if e == 0:
                multiply_blocks(e, 0, quantise(pair[:, N:, :], "single"), 0)
            else:
                quantised = quantise(pair[:], "pair")
                multiply_blocks(e - 1, 2, quantised, 0)
                multiply_blocks(e, 0, quantised, N)
                for h in range(BLOCKS):
                    activate(e - 1, h)
            multiply_blocks(e, 1, quantise(single[:], "single"), 0)
            if e + EARLY < len(gathers):
                gather_tokens(e + EARLY)
            pair = next_pair
        interleave(nc.vector.tensor_copy, pair[:, N:, :], raw[WHOLE, 0])
        quantised = quantise(pair[:], "pair")
        multiply_blocks(WHOLE - 1, 2, quantised, 0)
        multiply_blocks(WHOLE, 0, quantised, N)
        for h in range(BLOCKS):
            activate(WHOLE - 1, h)
        for index in range(WHOLE * PASSES + 1, E * PASSES - 1):
            e, o = divmod(index, PASSES)
            single = single_tile(N)
            interleave(nc.scalar.copy if index % 2 else nc.vector.tensor_copy, single[:], raw[e, o])
            multiply_blocks(e, o, quantise(single[:], "single"), 0)
            if o == PASSES - 1:
                for h in range(BLOCKS):
                    activate(e, h)
        halves = [single_tile(P) for h in range(BLOCKS)]
        for h, copy in enumerate((nc.scalar.copy, nc.vector.tensor_copy)):
            interleave(copy, halves[h][:], raw[last, 2][:, :, h * P : (h + 1) * P])
        for h in range(BLOCKS):
            multiply(last, 2, h, quantise(halves[h][:], "single"), 0)
            activate(last, h)

        def gated(h, r, tokens, name):
            width = tokens.stop - tokens.start
            term = prod_pool.tile([P, width], F32, name=name)
            entries = back_lists[r][:, tokens.start // 16 : tokens.stop // 16]
            nc.vector.tensor_tensor(term[:], results[h][:].indirect(entries), gates[r][:, tokens], MULT)
            return term

        turned = [psum.tile([P, P], F32, name="acc", tag="acc") for i in range(T // P)]
        for r in range(TOP):
            term = gated(0, r, slice(0, T), "first%d" % r)
            for i in range(T // P):
                nc.tensor.matmul(
                    turned[i][:], term[:, i * P : (i + 1) * P], identity[:],
                    start=(r == 0), stop=(r == TOP - 1), is_transpose=True,
                )
        back = psum.tile([P, T], F32, name="acc", tag="acc")
        for i in range(T // P):
            by_token = prod_pool.tile([P, P], F32, name="by_token%d" % i)
            nc.scalar.copy(by_token[:], turned[i][:])
            nc.tensor.transpose(back[:, i * P : (i + 1) * P], by_token[:], identity[:])
        total = prod_pool.tile([P, T], F32, name="total")
        nc.scalar.copy(total[:], back[:])
        nc.sync.dma_start(out[0:P, :], total[:])

        left, right = slice(0, T // 2), slice(T // 2, T)
        terms = [gated(1, r, slice(0, T), "second%d" % r) for r in range(TOP - 1)]
        third_left = gated(1, TOP - 1, left, "third_left")
        partial = prod_pool.tile([P, T], F32, name="partial")
        nc.vector.tensor_tensor(partial[:], terms[0][:], terms[1][:], ADD)
        third_right = gated(1, TOP - 1, right, "third_right")
        for name, tokens, third in (("left", left, third_left), ("right", right, third_right)):
            done = prod_pool.tile([P, T // 2], F32, name=name)
            nc.vector.tensor_tensor(done[:], partial[:, tokens], third[:], ADD)
            nc.sync.dma_start(out[P : 2 * P, tokens], done[:])
